import numpy as np
import ml_dtypes


def mxq(x, axis, fmt="e4m3"):
    dtype, down = {"e4m3": (ml_dtypes.float8_e4m3fn, 7), "e5m2": (ml_dtypes.float8_e5m2, 14)}[fmt]
    v = np.moveaxis(np.asarray(x, np.float32).astype(ml_dtypes.bfloat16).astype(np.float64), axis, -1)
    blocks = v.reshape(v.shape[:-1] + (-1, 32))
    amax = np.abs(blocks).max(-1, keepdims=True)
    byte = np.maximum(np.where(amax > 0, np.frexp(amax)[1] - 1 + 127, 0) - down, 1)
    scale = np.exp2(byte - 127.0)
    codes = (blocks / scale).astype(np.float32).astype(dtype).astype(np.float64)
    return np.moveaxis((codes * scale).reshape(v.shape), -1, axis)


WIDE = False


def mx_kscale(k):
    if not WIDE:
        return np.ones(k)
    levels = np.array([10, -10, 5, -5, 0])
    if k % 512:
        return np.exp2(np.random.permutation(np.resize(levels, k // 32))).repeat(32)
    a = np.empty((k // 512, 16))
    for p in range(k // 512):
        a[p, :8] = np.random.permutation(np.resize(levels, 8))
        for g in range(8):
            far = levels[np.abs(levels - a[p, g]) >= 10]
            a[p, g + 8] = far[np.random.randint(len(far))]
    return np.exp2(a.ravel()).repeat(32)


def f64(x):
    return np.asarray(x).astype(np.float64)


def striped(idx):
    return np.tile(idx.reshape(-1, 16).T, (8, 1)).astype(np.uint16)


def unstriped(offs):
    return offs[:16].T.reshape(-1).astype(np.int64)


def pack_weight(w):
    k, n = w.shape
    w = f64(np.asarray(w, np.float32).astype(ml_dtypes.bfloat16)).reshape(k // 32, 32, n)
    amax = np.abs(w).max(1)
    byte = np.clip(np.where(amax > 0, np.frexp(amax)[1] - 1 + 127 - 7, 1), 1, 254)
    scaled = (w * np.exp2(127.0 - byte)[:, None, :]).reshape(k, n).astype(np.float32)
    words = np.ascontiguousarray(scaled.reshape(k // 512, 128, 4, n).transpose(0, 1, 3, 2)).astype(ml_dtypes.float8_e4m3fn).view(np.uint8)
    return words, np.ascontiguousarray(byte.astype(np.uint8).reshape(k // 512, 16, n))


def unpack_weight(words, scales):
    g, p, n, _ = words.shape
    vals = np.ascontiguousarray(words).view(ml_dtypes.float8_e4m3fn).astype(np.float64) * np.repeat(np.exp2(scales.astype(np.float64) - 127.0), 8, axis=1)[..., None]
    return vals.transpose(0, 1, 3, 2).reshape(g * 512, n)


def relu(v):
    return np.maximum(v, 0.0)


K, T, D, S, V, N = 1536, 512, 4, 1024, 256, 256


def setup_inputs():
    n = np.random.standard_normal
    s = mx_kscale(K)[:, None]
    words, scales = pack_weight(n((K, N)) / np.sqrt(K) / s)
    return {
        "xT": (n((K, T)) * s).astype(np.float32),
        "w_words": words,
        "w_scales": scales,
        "b": (0.3 * n((N, 1))).astype(np.float32),
        "gate": np.tile(np.random.uniform(0.2, 1.0, (D, 1, V)) / np.sqrt(D), (1, N, 1)).astype(np.float32),
        "pos1": striped(np.random.permutation(T)[:V]),
        "pos2": striped(np.random.permutation(T)[:V]),
        "pos3": striped(np.random.permutation(T)[:V]),
        "pos4": striped(np.random.permutation(T)[:V]),
    }


def reference(xT, w_words, w_scales, b, gate, pos1, pos2, pos3, pos4):
    w = unpack_weight(w_words, w_scales)
    y = w.T @ mxq(f64(xT), 0, "e4m3")
    y = relu(y + f64(b))
    return sum(f64(gate[d]) * y[:, unstriped(p)] for d, p in enumerate((pos1, pos2, pos3, pos4)))

@@ -1,0 +1,162 @@
+from contextlib import ExitStack
+
+import concourse.mybir as mybir
+
+K, T, D, V, N = 1536, 512, 4, 256, 256
+FLOPS = 2 * K * T * N
+
+F32 = mybir.dt.float32
+BF16 = mybir.dt.bfloat16
+I32 = mybir.dt.int32
+U32 = mybir.dt.uint32
+U16 = mybir.dt.uint16
+U8 = mybir.dt.uint8
+FP8X4 = mybir.dt.float8_e4m3fn_x4
+RELU = mybir.ActivationFunctionType.Relu
+ADD, MULT, MAX = mybir.AluOpType.add, mybir.AluOpType.mult, mybir.AluOpType.max
+
+P = 128
+PACK = 4
+PASSES = K // (P * PACK)
+BLOCKS = N // P
+
+CHUNKS = ((0, 0, 512), (1, 0, 512), (2, 0, 384), (2, 384, 128))
+GROUPS = ((0, 256), (256, 128), (384, 128))
+
+
+def tile_picked_agg_lin_relu_sub_l_kernel(tc, xT, w_words, w_scales, b, gate, pos1, pos2, pos3, pos4, out):
+    nc = tc.nc
+    with ExitStack() as ctx:
+        keep = ctx.enter_context(tc.tile_pool(name="keep", bufs=1))
+        psum = ctx.enter_context(tc.psum_pool(name="psum", bufs=1))
+
+        lists = [keep.tile([P, V // 16], U16, name=f"list{d}") for d in range(D)]
+        raw = [keep.tile([P, PACK, n], F32, name=f"raw{i}") for i, (a, t0, n) in enumerate(CHUNKS)]
+        grouped = [keep.tile([P, n, PACK], BF16, align_bytes=64, name=f"grouped{i}") for i, (a, t0, n) in enumerate(CHUNKS)]
+        codes = [keep.tile([P, n], U32, align_bytes=64, name=f"codes{i}") for i, (a, t0, n) in enumerate(CHUNKS)]
+        scales = [keep.tile([P, n], U8, align_bytes=64, name=f"scales{i}") for i, (a, t0, n) in enumerate(CHUNKS)]
+        w_sb = [keep.tile([P, PASSES, P * PACK], U8, align_bytes=64, name=f"w_sb{m}") for m in range(BLOCKS)]
+        w_sc = keep.tile([P, PASSES, N], U8, align_bytes=64, name="w_sc")
+        bias = keep.tile([P, BLOCKS], F32, name="bias")
+        gates = [keep.tile([P, D, V], F32, name=f"gates{m}") for m in range(BLOCKS)]
+        y = [keep.tile([P, T], F32, name=f"y{m}") for m in range(BLOCKS)]
+        picked = [keep.tile([P, D, V], F32, name=f"picked{m}") for m in range(BLOCKS)]
+        half = [keep.tile([P, 2, V], F32, name=f"half{m}") for m in range(BLOCKS)]
+        result = [keep.tile([P, V], F32, name=f"result{m}") for m in range(BLOCKS)]
+        warm = keep.tile([P, 8], F32, name="warm")
+        acc = [[psum.tile([P, n], F32, name=f"acc{m}_{g}") for g, (t0, n) in enumerate(GROUPS)] for m in range(BLOCKS)]
+
+        x_rows = xT.rearrange("(a p j) t -> a p j t", p=P, j=PACK)
+
+        def load(i):
+            a, t0, n = CHUNKS[i]
+            nc.sync.dma_start(out=raw[i][:], in_=x_rows[a][:, :, t0 : t0 + n])
+
+        def interleave(copy, i, c0, c1):
+            copy(
+                out=grouped[i][:, c0:c1, :].rearrange("p (c i) j -> p c j i", i=4),
+                in_=raw[i][:, :, c0:c1].rearrange("p j (c i) -> p c j i", i=4),
+            )
+
+        def quantize(i, c0, c1):
+            nc.vector.quantize_mx(
+                out=codes[i][:, c0:c1].bitcast(FP8X4),
+                scales=scales[i][:, c0:c1],
+                in_=grouped[i][:, c0:c1, :].rearrange("p c j -> p (c j)"),
+            )
+
+        def multiply(i, g, m):
+            a, c0, cn = CHUNKS[i]
+            t0, n = GROUPS[g]
+            s = slice(t0 - c0, t0 - c0 + n)
+            nc.tensor.matmul_mx(
+                out=acc[m][g][:],
+                lhsT=w_sb[m][:, a, :].bitcast(FP8X4),
+                lhsT_scale=w_sc[:, a, m * P : (m + 1) * P],
+                rhs=codes[i][:, s].bitcast(FP8X4),
+                rhs_scale=scales[i][:, s],
+                start=(a == 0),
+                stop=(a == PASSES - 1),
+            )
+
+        def finish_scalar(g, m):
+            t0, n = GROUPS[g]
+            nc.scalar.activation(out=y[m][:, t0 : t0 + n], in_=acc[m][g][:], func=RELU, bias=bias[:, m : m + 1], scale=1.0)
+
+        def finish_vector(g, m):
+            t0, n = GROUPS[g]
+            nc.vector.tensor_scalar(out=y[m][:, t0 : t0 + n], in0=acc[m][g][:], scalar1=bias[:, m : m + 1], scalar2=0.0, op0=ADD, op1=MAX)
+
+        def gather(m, d):
+            nc.vector.tensor_tensor(picked[m][:, d, :], y[m][:].indirect(lists[d][:]), gates[m][:, d, :], MULT)
+
+        def store(m, v0=0, v1=V):
+            nc.sync.dma_start(out=out[m * P : (m + 1) * P, v0:v1], in_=result[m][:, v0:v1])
+
+        nc.vector.memset(w_sc[:].rearrange("p a n -> p (a n)").bitcast(I32), 0)
+        nc.vector.memset(warm[:], 0.0)
+
+        def load_w(m):
+            nc.sync.dma_start(out=w_sb[m][:], in_=w_words[:, :, m * P : (m + 1) * P, :].rearrange("a p n r -> p a (n r)"))
+
+        def load_gate(m):
+            nc.sync.dma_start(out=gates[m][:], in_=gate[:, m * P : (m + 1) * P, :].rearrange("d p v -> p d v"))
+
+        for q in range(4):
+            nc.scalar.dma_start(
+                out=w_sc[32 * q : 32 * q + 4, :, :].bitcast(I32),
+                in_=w_scales[:, 4 * q : 4 * q + 4, :].rearrange("a r n -> r a n").bitcast(I32),
+            )
+        nc.scalar.dma_start(out=bias[:], in_=b.rearrange("(m p) o -> p (m o)", p=P))
+        load(0)
+        load(1)
+        load_w(0)
+        for i in range(2, len(CHUNKS)):
+            load(i)
+        load_gate(0)
+        for tile, pos in zip(lists, (pos1, pos2, pos3, pos4)):
+            nc.sync.dma_start(tile[:], pos)
+        load_w(1)
+        load_gate(1)
+
+        nc.scalar.activation(out=warm[:, 0:1], in_=warm[:, 1:2], func=RELU)
+
+        interleave(nc.scalar.copy, 0, 0, 512)
+        interleave(nc.vector.tensor_copy, 1, 0, 512)
+        quantize(0, 0, 512)
+        for g in range(3):
+            multiply(0, g, 0)
+        quantize(1, 0, 512)
+        for g in range(3):
+            multiply(1, g, 0)
+        interleave(nc.vector.tensor_copy, 2, 0, 256)
+        interleave(nc.scalar.copy, 2, 256, 384)
+        quantize(2, 0, 256)
+        multiply(2, 0, 0)
+        finish_scalar(0, 0)
+        quantize(2, 256, 384)
+        multiply(2, 1, 0)
+        finish_scalar(1, 0)
+        interleave(nc.vector.tensor_copy, 3, 0, 128)
+        quantize(3, 0, 128)
+        multiply(3, 2, 0)
+        finish_scalar(2, 0)
+        for g in range(3):
+            for i in (0, 1, 2 if g < 2 else 3):
+                multiply(i, g, 1)
+            finish_scalar(g, 1)
+
+
+        for d in range(D):
+            gather(0, d)
+        gather(1, 0)
+        nc.vector.tensor_tensor(half[0][:], picked[0][:, 0:2, :], picked[0][:, 2:4, :], ADD)
+        gather(1, 1)
+        nc.vector.tensor_tensor(result[0][:], half[0][:, 0, :], half[0][:, 1, :], ADD)
+        store(0)
+        gather(1, 2)
+        nc.vector.tensor_tensor(half[1][:, 0, :], picked[1][:, 0, :], picked[1][:, 1, :], ADD)
+        nc.vector.tensor_tensor(half[1][:, 1, :], half[1][:, 0, :], picked[1][:, 2, :], ADD)
+        gather(1, 3)
+        nc.vector.tensor_tensor(result[1][:], half[1][:, 1, :], picked[1][:, 3, :], ADD)
+        store(1)

@@ -102,13 +102,13 @@ def tile_picked_agg_lin_relu_sub_l_kernel(tc, xT, w_words, w_scales, b, gate, po
         def load_gate(m):
             nc.sync.dma_start(out=gates[m][:], in_=gate[:, m * P : (m + 1) * P, :].rearrange("d p v -> p d v"))
 
+        nc.scalar.dma_start(out=bias[:], in_=b.rearrange("(m p) o -> p (m o)", p=P))
+        load(0)
         for q in range(4):
-            nc.scalar.dma_start(
+            nc.sync.dma_start(
                 out=w_sc[32 * q : 32 * q + 4, :, :].bitcast(I32),
                 in_=w_scales[:, 4 * q : 4 * q + 4, :].rearrange("a r n -> r a n").bitcast(I32),
             )
-        nc.scalar.dma_start(out=bias[:], in_=b.rearrange("(m p) o -> p (m o)", p=P))
-        load(0)
         load(1)
         load_w(0)
         for i in range(2, len(CHUNKS)):
@@ -121,26 +121,24 @@ def tile_picked_agg_lin_relu_sub_l_kernel(tc, xT, w_words, w_scales, b, gate, po
 
         nc.scalar.activation(out=warm[:, 0:1], in_=warm[:, 1:2], func=RELU)
 
-        interleave(nc.scalar.copy, 0, 0, 512)
-        interleave(nc.vector.tensor_copy, 1, 0, 512)
-        quantize(0, 0, 512)
-        for g in range(3):
-            multiply(0, g, 0)
-        quantize(1, 0, 512)
-        for g in range(3):
-            multiply(1, g, 0)
+        for i in (0, 1):
+            interleave(nc.vector.tensor_copy, i, 0, 320)
+            interleave(nc.scalar.copy, i, 320, 512)
+            quantize(i, 0, 512)
+            for g in range(3):
+                multiply(i, g, 0)
         interleave(nc.vector.tensor_copy, 2, 0, 256)
         interleave(nc.scalar.copy, 2, 256, 384)
+        interleave(nc.scalar.copy, 3, 0, 128)
         quantize(2, 0, 256)
         multiply(2, 0, 0)
         finish_scalar(0, 0)
         quantize(2, 256, 384)
         multiply(2, 1, 0)
         finish_scalar(1, 0)
-        interleave(nc.vector.tensor_copy, 3, 0, 128)
         quantize(3, 0, 128)
         multiply(3, 2, 0)
-        finish_scalar(2, 0)
+        finish_vector(2, 0)
         for g in range(3):
             for i in (0, 1, 2 if g < 2 else 3):
                 multiply(i, g, 1)

@@ -96,13 +96,12 @@ def tile_picked_agg_lin_relu_sub_l_kernel(tc, xT, w_words, w_scales, b, gate, po
         nc.vector.memset(w_sc[:].rearrange("p a n -> p (a n)").bitcast(I32), 0)
         nc.vector.memset(warm[:], 0.0)
 
-        def load_w(m):
-            nc.sync.dma_start(out=w_sb[m][:], in_=w_words[:, :, m * P : (m + 1) * P, :].rearrange("a p n r -> p a (n r)"))
+        def load_w(m, a0, a1):
+            nc.sync.dma_start(out=w_sb[m][:, a0:a1, :], in_=w_words[a0:a1, :, m * P : (m + 1) * P, :].rearrange("a p n r -> p a (n r)"))
 
         def load_gate(m):
             nc.sync.dma_start(out=gates[m][:], in_=gate[:, m * P : (m + 1) * P, :].rearrange("d p v -> p d v"))
 
-        nc.scalar.dma_start(out=bias[:], in_=b.rearrange("(m p) o -> p (m o)", p=P))
         load(0)
         for q in range(4):
             nc.sync.dma_start(
@@ -110,13 +109,15 @@ def tile_picked_agg_lin_relu_sub_l_kernel(tc, xT, w_words, w_scales, b, gate, po
                 in_=w_scales[:, 4 * q : 4 * q + 4, :].rearrange("a r n -> r a n").bitcast(I32),
             )
         load(1)
-        load_w(0)
+        load_w(0, 0, 2)
         for i in range(2, len(CHUNKS)):
             load(i)
+        load_w(0, 2, 3)
+        nc.sync.dma_start(out=bias[:], in_=b.rearrange("(m p) o -> p (m o)", p=P))
         load_gate(0)
         for tile, pos in zip(lists, (pos1, pos2, pos3, pos4)):
             nc.sync.dma_start(tile[:], pos)
-        load_w(1)
+        load_w(1, 0, 3)
         load_gate(1)
 
         nc.scalar.activation(out=warm[:, 0:1], in_=warm[:, 1:2], func=RELU)
@@ -129,10 +130,11 @@ def tile_picked_agg_lin_relu_sub_l_kernel(tc, xT, w_words, w_scales, b, gate, po
                 multiply(i, g, 0)
         interleave(nc.vector.tensor_copy, 2, 0, 256)
         interleave(nc.scalar.copy, 2, 256, 384)
-        interleave(nc.scalar.copy, 3, 0, 128)
+        interleave(nc.scalar.copy, 3, 64, 128)
         quantize(2, 0, 256)
         multiply(2, 0, 0)
         finish_scalar(0, 0)
+        interleave(nc.vector.tensor_copy, 3, 0, 64)
         quantize(2, 256, 384)
         multiply(2, 1, 0)
         finish_scalar(1, 0)

@@ -21,7 +21,7 @@ PASSES = K // (P * PACK)
 BLOCKS = N // P
 
 CHUNKS = ((0, 0, 512), (1, 0, 512), (2, 0, 384), (2, 384, 128))
-GROUPS = ((0, 256), (256, 128), (384, 128))
+GROUPS = ((0, 128), (128, 256), (384, 128))
 
 
 def tile_picked_agg_lin_relu_sub_l_kernel(tc, xT, w_words, w_scales, b, gate, pos1, pos2, pos3, pos4, out):
@@ -99,8 +99,11 @@ def tile_picked_agg_lin_relu_sub_l_kernel(tc, xT, w_words, w_scales, b, gate, po
         def load_w(m, a0, a1):
             nc.sync.dma_start(out=w_sb[m][:, a0:a1, :], in_=w_words[a0:a1, :, m * P : (m + 1) * P, :].rearrange("a p n r -> p a (n r)"))
 
-        def load_gate(m):
-            nc.sync.dma_start(out=gates[m][:], in_=gate[:, m * P : (m + 1) * P, :].rearrange("d p v -> p d v"))
+        def load_gate(m, d0, d1):
+            nc.sync.dma_start(out=gates[m][:, d0:d1, :], in_=gate[d0:d1, m * P : (m + 1) * P, :].rearrange("d p v -> p d v"))
+
+        def load_list(d):
+            nc.sync.dma_start(lists[d][:], (pos1, pos2, pos3, pos4)[d])
 
         load(0)
         for q in range(4):
@@ -114,11 +117,14 @@ def tile_picked_agg_lin_relu_sub_l_kernel(tc, xT, w_words, w_scales, b, gate, po
             load(i)
         load_w(0, 2, 3)
         nc.sync.dma_start(out=bias[:], in_=b.rearrange("(m p) o -> p (m o)", p=P))
-        load_gate(0)
-        for tile, pos in zip(lists, (pos1, pos2, pos3, pos4)):
-            nc.sync.dma_start(tile[:], pos)
+        load_list(0)
+        load_gate(0, 0, 2)
+        load_list(1)
+        load_gate(0, 2, 4)
         load_w(1, 0, 3)
-        load_gate(1)
+        load_list(2)
+        load_list(3)
+        load_gate(1, 0, 4)
 
         nc.scalar.activation(out=warm[:, 0:1], in_=warm[:, 1:2], func=RELU)
 
@@ -128,19 +134,20 @@ def tile_picked_agg_lin_relu_sub_l_kernel(tc, xT, w_words, w_scales, b, gate, po
             quantize(i, 0, 512)
             for g in range(3):
                 multiply(i, g, 0)
-        interleave(nc.vector.tensor_copy, 2, 0, 256)
+        interleave(nc.vector.tensor_copy, 2, 0, 128)
         interleave(nc.scalar.copy, 2, 256, 384)
+        interleave(nc.vector.tensor_copy, 2, 128, 256)
         interleave(nc.scalar.copy, 3, 64, 128)
-        quantize(2, 0, 256)
+        quantize(2, 0, 128)
         multiply(2, 0, 0)
-        finish_scalar(0, 0)
         interleave(nc.vector.tensor_copy, 3, 0, 64)
-        quantize(2, 256, 384)
+        quantize(2, 128, 384)
         multiply(2, 1, 0)
-        finish_scalar(1, 0)
+        finish_scalar(0, 0)
         quantize(3, 0, 128)
         multiply(3, 2, 0)
-        finish_vector(2, 0)
+        finish_scalar(1, 0)
+        finish_scalar(2, 0)
         for g in range(3):
             for i in (0, 1, 2 if g < 2 else 3):
                 multiply(i, g, 1)
@@ -150,13 +157,13 @@ def tile_picked_agg_lin_relu_sub_l_kernel(tc, xT, w_words, w_scales, b, gate, po
         for d in range(D):
             gather(0, d)
         gather(1, 0)
-        nc.vector.tensor_tensor(half[0][:], picked[0][:, 0:2, :], picked[0][:, 2:4, :], ADD)
         gather(1, 1)
-        nc.vector.tensor_tensor(result[0][:], half[0][:, 0, :], half[0][:, 1, :], ADD)
-        store(0)
+        nc.vector.tensor_tensor(half[0][:], picked[0][:, 0:2, :], picked[0][:, 2:4, :], ADD)
         gather(1, 2)
         nc.vector.tensor_tensor(half[1][:, 0, :], picked[1][:, 0, :], picked[1][:, 1, :], ADD)
-        nc.vector.tensor_tensor(half[1][:, 1, :], half[1][:, 0, :], picked[1][:, 2, :], ADD)
         gather(1, 3)
+        nc.vector.tensor_tensor(half[1][:, 1, :], half[1][:, 0, :], picked[1][:, 2, :], ADD)
+        nc.vector.tensor_tensor(result[0][:], half[0][:, 0, :], half[0][:, 1, :], ADD)
+        store(0)
         nc.vector.tensor_tensor(result[1][:], half[1][:, 1, :], picked[1][:, 3, :], ADD)
         store(1)

@@ -1,6 +1,7 @@
 from contextlib import ExitStack
 
 import concourse.mybir as mybir
+from concourse.masks import make_identity
 
 K, T, D, V, N = 1536, 512, 4, 256, 256
 FLOPS = 2 * K * T * N
@@ -38,6 +39,9 @@ def tile_picked_agg_lin_relu_sub_l_kernel(tc, xT, w_words, w_scales, b, gate, po
         w_sb = [keep.tile([P, PASSES, P * PACK], U8, align_bytes=64, name=f"w_sb{m}") for m in range(BLOCKS)]
         w_sc = keep.tile([P, PASSES, N], U8, align_bytes=64, name="w_sc")
         bias = keep.tile([P, BLOCKS], F32, name="bias")
+        identity = keep.tile([P, P], F32, name="identity")
+        bias_rows = keep.tile([P, P], F32, name="bias_rows")
+        bias_psum = psum.tile([P, P], F32, name="bias_psum")
         gates = [keep.tile([P, D, V], F32, name=f"gates{m}") for m in range(BLOCKS)]
         y = [keep.tile([P, T], F32, name=f"y{m}") for m in range(BLOCKS)]
         picked = [keep.tile([P, D, V], F32, name=f"picked{m}") for m in range(BLOCKS)]
@@ -105,6 +109,9 @@ def tile_picked_agg_lin_relu_sub_l_kernel(tc, xT, w_words, w_scales, b, gate, po
         def load_list(d):
             nc.sync.dma_start(lists[d][:], (pos1, pos2, pos3, pos4)[d])
 
+        make_identity(nc, identity[:])
+        nc.vector.memset(bias_rows[:], 0.0)
+        nc.scalar.dma_start(out=bias_rows[0:BLOCKS, :], in_=b.rearrange("(m p) o -> m (p o)", p=P))
         load(0)
         for q in range(4):
             nc.sync.dma_start(
@@ -116,15 +123,17 @@ def tile_picked_agg_lin_relu_sub_l_kernel(tc, xT, w_words, w_scales, b, gate, po
         for i in range(2, len(CHUNKS)):
             load(i)
         load_w(0, 2, 3)
-        nc.sync.dma_start(out=bias[:], in_=b.rearrange("(m p) o -> p (m o)", p=P))
         load_list(0)
-        load_gate(0, 0, 2)
         load_list(1)
-        load_gate(0, 2, 4)
+        load_gate(0, 0, 2)
         load_w(1, 0, 3)
         load_list(2)
+        load_gate(0, 2, 4)
         load_list(3)
-        load_gate(1, 0, 4)
+        load_gate(1, 0, 2)
+        load_gate(1, 2, 4)
+        nc.tensor.transpose(bias_psum[:], bias_rows[:], identity[:])
+        nc.vector.tensor_copy(out=bias[:], in_=bias_psum[:, 0:BLOCKS])
 
         nc.scalar.activation(out=warm[:, 0:1], in_=warm[:, 1:2], func=RELU)
 

from contextlib import ExitStack

import concourse.mybir as mybir
from concourse.masks import make_identity

K, T, D, V, N = 1536, 512, 4, 256, 256
FLOPS = 2 * K * T * N

F32 = mybir.dt.float32
BF16 = mybir.dt.bfloat16
I32 = mybir.dt.int32
U32 = mybir.dt.uint32
U16 = mybir.dt.uint16
U8 = mybir.dt.uint8
FP8X4 = mybir.dt.float8_e4m3fn_x4
RELU = mybir.ActivationFunctionType.Relu
ADD, MULT, MAX = mybir.AluOpType.add, mybir.AluOpType.mult, mybir.AluOpType.max

P = 128
PACK = 4
PASSES = K // (P * PACK)
BLOCKS = N // P

CHUNKS = ((0, 0, 512), (1, 0, 512), (2, 0, 384), (2, 384, 128))
GROUPS = ((0, 128), (128, 256), (384, 128))


def tile_picked_agg_lin_relu_sub_l_kernel(tc, xT, w_words, w_scales, b, gate, pos1, pos2, pos3, pos4, out):
    nc = tc.nc
    with ExitStack() as ctx:
        keep = ctx.enter_context(tc.tile_pool(name="keep", bufs=1))
        psum = ctx.enter_context(tc.psum_pool(name="psum", bufs=1))

        lists = [keep.tile([P, V // 16], U16, name=f"list{d}") for d in range(D)]
        raw = [keep.tile([P, PACK, n], F32, name=f"raw{i}") for i, (a, t0, n) in enumerate(CHUNKS)]
        grouped = [keep.tile([P, n, PACK], BF16, align_bytes=64, name=f"grouped{i}") for i, (a, t0, n) in enumerate(CHUNKS)]
        codes = [keep.tile([P, n], U32, align_bytes=64, name=f"codes{i}") for i, (a, t0, n) in enumerate(CHUNKS)]
        scales = [keep.tile([P, n], U8, align_bytes=64, name=f"scales{i}") for i, (a, t0, n) in enumerate(CHUNKS)]
        w_sb = [keep.tile([P, PASSES, P * PACK], U8, align_bytes=64, name=f"w_sb{m}") for m in range(BLOCKS)]
        w_sc = keep.tile([P, PASSES, N], U8, align_bytes=64, name="w_sc")
        bias = keep.tile([P, BLOCKS], F32, name="bias")
        identity = keep.tile([P, P], F32, name="identity")
        bias_rows = keep.tile([P, P], F32, name="bias_rows")
        bias_psum = psum.tile([P, P], F32, name="bias_psum")
        gates = [keep.tile([P, D, V], F32, name=f"gates{m}") for m in range(BLOCKS)]
        y = [keep.tile([P, T], F32, name=f"y{m}") for m in range(BLOCKS)]
        picked = [keep.tile([P, D, V], F32, name=f"picked{m}") for m in range(BLOCKS)]
        half = [keep.tile([P, 2, V], F32, name=f"half{m}") for m in range(BLOCKS)]
        result = [keep.tile([P, V], F32, name=f"result{m}") for m in range(BLOCKS)]
        warm = keep.tile([P, 8], F32, name="warm")
        acc = [[psum.tile([P, n], F32, name=f"acc{m}_{g}") for g, (t0, n) in enumerate(GROUPS)] for m in range(BLOCKS)]

        x_rows = xT.rearrange("(a p j) t -> a p j t", p=P, j=PACK)

        def load(i):
            a, t0, n = CHUNKS[i]
            nc.sync.dma_start(out=raw[i][:], in_=x_rows[a][:, :, t0 : t0 + n])

        def interleave(copy, i, c0, c1):
            copy(
                out=grouped[i][:, c0:c1, :].rearrange("p (c i) j -> p c j i", i=4),
                in_=raw[i][:, :, c0:c1].rearrange("p j (c i) -> p c j i", i=4),
            )

        def quantize(i, c0, c1):
            nc.vector.quantize_mx(
                out=codes[i][:, c0:c1].bitcast(FP8X4),
                scales=scales[i][:, c0:c1],
                in_=grouped[i][:, c0:c1, :].rearrange("p c j -> p (c j)"),
            )

        def multiply(i, g, m):
            a, c0, cn = CHUNKS[i]
            t0, n = GROUPS[g]
            s = slice(t0 - c0, t0 - c0 + n)
            nc.tensor.matmul_mx(
                out=acc[m][g][:],
                lhsT=w_sb[m][:, a, :].bitcast(FP8X4),
                lhsT_scale=w_sc[:, a, m * P : (m + 1) * P],
                rhs=codes[i][:, s].bitcast(FP8X4),
                rhs_scale=scales[i][:, s],
                start=(a == 0),
                stop=(a == PASSES - 1),
            )

        def finish_scalar(g, m):
            t0, n = GROUPS[g]
            nc.scalar.activation(out=y[m][:, t0 : t0 + n], in_=acc[m][g][:], func=RELU, bias=bias[:, m : m + 1], scale=1.0)

        def finish_vector(g, m):
            t0, n = GROUPS[g]
            nc.vector.tensor_scalar(out=y[m][:, t0 : t0 + n], in0=acc[m][g][:], scalar1=bias[:, m : m + 1], scalar2=0.0, op0=ADD, op1=MAX)

        def gather(m, d):
            nc.vector.tensor_tensor(picked[m][:, d, :], y[m][:].indirect(lists[d][:]), gates[m][:, d, :], MULT)

        def store(m, v0=0, v1=V):
            nc.sync.dma_start(out=out[m * P : (m + 1) * P, v0:v1], in_=result[m][:, v0:v1])

        nc.vector.memset(w_sc[:].rearrange("p a n -> p (a n)").bitcast(I32), 0)
        nc.vector.memset(warm[:], 0.0)

        def load_w(m, a0, a1):
            nc.sync.dma_start(out=w_sb[m][:, a0:a1, :], in_=w_words[a0:a1, :, m * P : (m + 1) * P, :].rearrange("a p n r -> p a (n r)"))

        def load_gate(m, d0, d1):
            nc.sync.dma_start(out=gates[m][:, d0:d1, :], in_=gate[d0:d1, m * P : (m + 1) * P, :].rearrange("d p v -> p d v"))

        def load_list(d):
            nc.sync.dma_start(lists[d][:], (pos1, pos2, pos3, pos4)[d])

        make_identity(nc, identity[:])
        nc.vector.memset(bias_rows[:], 0.0)
        nc.scalar.dma_start(out=bias_rows[0:BLOCKS, :], in_=b.rearrange("(m p) o -> m (p o)", p=P))
        load(0)
        for q in range(4):
            nc.sync.dma_start(
                out=w_sc[32 * q : 32 * q + 4, :, :].bitcast(I32),
                in_=w_scales[:, 4 * q : 4 * q + 4, :].rearrange("a r n -> r a n").bitcast(I32),
            )
        load(1)
        load_w(0, 0, 2)
        for i in range(2, len(CHUNKS)):
            load(i)
        load_w(0, 2, 3)
        load_list(0)
        load_list(1)
        load_gate(0, 0, 2)
        load_w(1, 0, 3)
        load_list(2)
        load_gate(0, 2, 4)
        load_list(3)
        load_gate(1, 0, 2)
        load_gate(1, 2, 4)
        nc.tensor.transpose(bias_psum[:], bias_rows[:], identity[:])
        nc.vector.tensor_copy(out=bias[:], in_=bias_psum[:, 0:BLOCKS])

        nc.scalar.activation(out=warm[:, 0:1], in_=warm[:, 1:2], func=RELU)

        for i in (0, 1):
            interleave(nc.vector.tensor_copy, i, 0, 320)
            interleave(nc.scalar.copy, i, 320, 512)
            quantize(i, 0, 512)
            for g in range(3):
                multiply(i, g, 0)
        interleave(nc.vector.tensor_copy, 2, 0, 128)
        interleave(nc.scalar.copy, 2, 256, 384)
        interleave(nc.vector.tensor_copy, 2, 128, 256)
        interleave(nc.scalar.copy, 3, 64, 128)
        quantize(2, 0, 128)
        multiply(2, 0, 0)
        interleave(nc.vector.tensor_copy, 3, 0, 64)
        quantize(2, 128, 384)
        multiply(2, 1, 0)
        finish_scalar(0, 0)
        quantize(3, 0, 128)
        multiply(3, 2, 0)
        finish_scalar(1, 0)
        finish_scalar(2, 0)
        for g in range(3):
            for i in (0, 1, 2 if g < 2 else 3):
                multiply(i, g, 1)
            finish_scalar(g, 1)


        for d in range(D):
            gather(0, d)
        gather(1, 0)
        gather(1, 1)
        nc.vector.tensor_tensor(half[0][:], picked[0][:, 0:2, :], picked[0][:, 2:4, :], ADD)
        gather(1, 2)
        nc.vector.tensor_tensor(half[1][:, 0, :], picked[1][:, 0, :], picked[1][:, 1, :], ADD)
        gather(1, 3)
        nc.vector.tensor_tensor(half[1][:, 1, :], half[1][:, 0, :], picked[1][:, 2, :], ADD)
        nc.vector.tensor_tensor(result[0][:], half[0][:, 0, :], half[0][:, 1, :], ADD)
        store(0)
        nc.vector.tensor_tensor(result[1][:], half[1][:, 1, :], picked[1][:, 3, :], ADD)
        store(1)
